import numpy as np
import ml_dtypes


def mxq(x, axis, fmt="e4m3"):
    dtype, down = {"e4m3": (ml_dtypes.float8_e4m3fn, 7), "e5m2": (ml_dtypes.float8_e5m2, 14)}[fmt]
    v = np.moveaxis(np.asarray(x, np.float32).astype(ml_dtypes.bfloat16).astype(np.float64), axis, -1)
    blocks = v.reshape(v.shape[:-1] + (-1, 32))
    amax = np.abs(blocks).max(-1, keepdims=True)
    byte = np.maximum(np.where(amax > 0, np.frexp(amax)[1] - 1 + 127, 0) - down, 1)
    scale = np.exp2(byte - 127.0)
    codes = (blocks / scale).astype(np.float32).astype(dtype).astype(np.float64)
    return np.moveaxis((codes * scale).reshape(v.shape), -1, axis)


WIDE = False


def mx_kscale(k):
    if not WIDE:
        return np.ones(k)
    levels = np.array([10, -10, 5, -5, 0])
    if k % 512:
        return np.exp2(np.random.permutation(np.resize(levels, k // 32))).repeat(32)
    a = np.empty((k // 512, 16))
    for p in range(k // 512):
        a[p, :8] = np.random.permutation(np.resize(levels, 8))
        for g in range(8):
            far = levels[np.abs(levels - a[p, g]) >= 10]
            a[p, g + 8] = far[np.random.randint(len(far))]
    return np.exp2(a.ravel()).repeat(32)


def f64(x):
    return np.asarray(x).astype(np.float64)


def striped8(idx):
    return np.asarray(idx).reshape(8, -1, 16).transpose(0, 2, 1).reshape(128, -1).astype(np.uint16)


def unstriped8(offs):
    return offs.reshape(8, 16, -1).transpose(0, 2, 1).reshape(8, -1).astype(np.int64)


def pick8(x, idx, run):
    r = np.arange(len(x))
    return x[r[:, None], idx[r % (8 * run) // run]]


E2M1 = np.array([0.0, 0.5, 1.0, 1.5, 2.0, 3.0, 4.0, 6.0, -0.0, -0.5, -1.0, -1.5, -2.0, -3.0, -4.0, -6.0])


def pack_weight(w, fmt):
    k, n = w.shape
    w = f64(np.asarray(w, np.float32).astype(ml_dtypes.bfloat16)).reshape(k // 32, 32, n)
    amax = np.abs(w).max(1)
    if fmt == "e4m3":
        byte = np.frexp(amax)[1] - 1 + 127 - 7
    else:
        mant, ex = np.frexp(amax / 6.0)
        byte = np.where(mant > 0.5, ex, ex - 1) + 127
    byte = np.clip(np.where(amax > 0, byte, 1), 1, 254)
    scaled = (w * np.exp2(127.0 - byte)[:, None, :]).reshape(k, n).astype(np.float32)
    by_word = np.ascontiguousarray(scaled.reshape(k // 512, 128, 4, n).transpose(0, 1, 3, 2))
    if fmt == "e4m3":
        words = by_word.astype(ml_dtypes.float8_e4m3fn).view(np.uint8)
    else:
        c = by_word.astype(ml_dtypes.float4_e2m1fn).view(np.uint8) & 0xF
        words = (c[..., 0::2] | (c[..., 1::2] << 4)).reshape(k // 512, 128, 2 * n)
    return np.ascontiguousarray(words), np.ascontiguousarray(byte.astype(np.uint8).reshape(k // 512, 16, n))


def unpack_weight(words, scales, fmt):
    g, _, n = scales.shape
    words = np.ascontiguousarray(words).reshape(g, 128, n, -1)
    if fmt == "e4m3":
        vals = words.view(ml_dtypes.float8_e4m3fn).astype(np.float64)
    else:
        nib = np.empty((g, 128, n, 4), np.uint8)
        nib[..., 0::2] = words & 0xF
        nib[..., 1::2] = words >> 4
        vals = E2M1[nib]
    vals = vals * np.repeat(np.exp2(scales.astype(np.float64) - 127.0), 8, axis=1)[..., None]
    return vals.transpose(0, 1, 3, 2).reshape(g * 512, n)


def sigmoid(v):
    return 1.0 / (1.0 + np.exp(-v))


D, V, Q, I = 512, 2048, 128, 512


def setup_inputs():
    n = np.random.standard_normal
    idx = np.stack([np.random.permutation(V)[:I] for _ in range(8)])
    idx2 = np.stack([np.random.permutation(V)[:I] for _ in range(8)])
    fd = mx_kscale(D)
    vocp = pack_weight(n((D, V)) / fd[:, None], "e4m3")
    return {
        "hid": (n((D, Q)) * 1.0 / np.sqrt(D) * fd[:, None]).astype(np.float32),
        "voc_words": vocp[0],
        "voc_scales": vocp[1],
        "margin": (np.random.uniform(0.0, 1.0, (1, I))).astype(np.float32),
        "steep": (np.random.uniform(1.0, 3.0, (Q, 1))).astype(np.float32),
        "dhid": (n((D, Q)) * 1.0 / np.sqrt(D) * fd[:, None]).astype(np.float32),
        "base": (0.5 * n((Q, V))).astype(np.float32),
        "offs": striped8(idx),
        "offs2": striped8(idx2),
    }


def reference(hid, voc_words, voc_scales, margin, steep, dhid, base, offs, offs2):
    idx = unstriped8(offs)
    idx2 = unstriped8(offs2)
    vocu = unpack_weight(voc_words, voc_scales, "e4m3")
    hidq = mxq(f64(hid), 0, "e4m3")
    a = hidq.T @ vocu
    dhidq = mxq(f64(dhid), 0, "e4m3")
    ta = dhidq.T @ vocu
    b = pick8(a, idx2, 16) - pick8(a, idx, 16)
    xb = pick8(ta, idx2, 16) - pick8(ta, idx, 16)
    xdb = xb * f64(steep) * sigmoid((b + f64(margin)) * f64(steep)) * (1.0 - sigmoid((b + f64(margin)) * f64(steep))) * f64(steep)
    xs1 = np.zeros((Q, V))
    xs1[np.arange(Q)[:, None], idx2[np.arange(Q) % 128 // 16]] = xdb
    xe2 = xdb * (-1.0)
    xs2 = np.zeros((Q, V))
    xs2[np.arange(Q)[:, None], idx[np.arange(Q) % 128 // 16]] = xe2
    xda = xs1 + xs2
    y = xda + f64(base)
    return y

@@ -1,0 +1,173 @@
+from contextlib import ExitStack
+
+import concourse.mybir as mybir
+from concourse.masks import make_identity
+
+D, V, Q, I = 512, 2048, 128, 512
+FLOPS = 2 * 2 * D * Q * V
+
+F32 = mybir.dt.float32
+BF16 = mybir.dt.bfloat16
+I32 = mybir.dt.int32
+U32 = mybir.dt.uint32
+U16 = mybir.dt.uint16
+U8 = mybir.dt.uint8
+FP8X4 = mybir.dt.float8_e4m3fn_x4
+ACT = mybir.ActivationFunctionType
+ALU = mybir.AluOpType
+
+P = 128
+PACK = 4
+CH = 512
+NCH = V // CH
+BLK = CH // P
+
+
+def tile_attend_hvpairmargin_heads_kernel(tc, hid, voc_words, voc_scales, margin, steep, dhid, base, offs, offs2, out):
+    nc = tc.nc
+    with ExitStack() as ctx:
+        lists = ctx.enter_context(tc.tile_pool(name="lists", bufs=1))
+        sb = ctx.enter_context(tc.tile_pool(name="sb", bufs=1))
+        ps = ctx.enter_context(tc.psum_pool(name="ps", bufs=1))
+
+        def bank(b, shape):
+            return ps.tile(shape, F32, name="bank%d" % b)
+
+        planes = sb.tile([P, CH], U8, name="planes", align_bytes=64)
+        nc.gpsimd.memset(planes[:].bitcast(I32), 0)
+        scales_i32 = voc_scales[0].bitcast(I32)
+        for quad in range(4):
+            nc.scalar.dma_start(
+                out=planes[32 * quad : 32 * quad + 16, :].bitcast(I32),
+                in_=scales_i32[4 * quad : 4 * quad + 4, :].rearrange("r (c n) -> c r n", c=NCH),
+            )
+        warm = sb.tile([P, 1], F32, name="warm")
+        warm_out = sb.tile([P, 1], F32, name="warm_out")
+        nc.gpsimd.memset(warm[:], 0.0)
+        nc.scalar.activation(warm_out[:], warm[:], ACT.Tanh)
+
+        hid_raw = sb.tile([P, PACK, Q], F32, name="hid_raw")
+        nc.sync.dma_start(out=hid_raw[:], in_=hid.rearrange("(p t) q -> p t q", t=PACK))
+        margin_cols = sb.tile([P, BLK], F32, name="margin_cols")
+        nc.sync.dma_start(out=margin_cols[:], in_=margin[0].rearrange("(p j) -> p j", j=BLK))
+        words_i32 = voc_words[0].rearrange("p n t -> p (n t)").bitcast(I32)
+        words = []
+        for c in range(NCH):
+            w = sb.tile([P, CH], U32, name="words%d" % c, align_bytes=64)
+            nc.sync.dma_start(out=w[:].bitcast(I32), in_=words_i32[:, c * CH : (c + 1) * CH])
+            words.append(w)
+        dhid_raw = sb.tile([P, PACK, Q], F32, name="dhid_raw")
+        nc.sync.dma_start(out=dhid_raw[:], in_=dhid.rearrange("(p t) q -> p t q", t=PACK))
+        first = lists.tile([P, I // 16], U16, name="first")
+        nc.sync.dma_start(first[:], offs)
+        second = lists.tile([P, I // 16], U16, name="second")
+        nc.sync.dma_start(second[:], offs2)
+        steep_col = sb.tile([P, 1], F32, name="steep_col")
+        nc.sync.dma_start(out=steep_col[:], in_=steep)
+        base_sb = []
+        for c in range(NCH):
+            t = sb.tile([P, CH], F32, name="base%d" % c)
+            nc.sync.dma_start(out=t[:], in_=base[:, c * CH : (c + 1) * CH])
+            base_sb.append(t)
+
+        ident = sb.tile([P, P], F32, name="ident")
+        make_identity(nc, ident[:])
+        xs1 = sb.tile([P, V], F32, name="xs1")
+        nc.vector.memset(xs1[:], 0.0)
+
+        def quantise(raw, tag):
+            grouped = sb.tile([P, Q, PACK], BF16, name=tag + "_bf16", tag=tag + "_stage", align_bytes=64)
+            nc.vector.tensor_copy(out=grouped[:], in_=raw[:].rearrange("p t q -> p q t"))
+            codes = sb.tile([P, Q], U32, name=tag + "_codes", align_bytes=64)
+            scale = sb.tile([P, Q], U8, name=tag + "_scale", align_bytes=64)
+            nc.vector.quantize_mx(
+                out=codes[:].bitcast(FP8X4), scales=scale[:], in_=grouped[:].rearrange("p q t -> p (q t)")
+            )
+            return codes, scale
+
+        def scores(codes, scale, first_bank, name):
+            table = sb.tile([P, V], F32, name=name)
+            for c in range(NCH):
+                acc = bank(first_bank + c, [P, CH])
+                nc.tensor.matmul_mx(
+                    out=acc[:],
+                    lhsT=codes[:].bitcast(FP8X4),
+                    lhsT_scale=scale[:],
+                    rhs=words[c][:].bitcast(FP8X4),
+                    rhs_scale=planes[4 * c : P, :],
+                    start=True,
+                    stop=True,
+                )
+                nc.scalar.copy(out=table[:, c * CH : (c + 1) * CH], in_=acc[:])
+            return table
+
+        hid_codes, hid_scale = quantise(hid_raw, "hid")
+        xs2 = sb.tile([P, V], F32, name="xs2", tag="hid_stage", align_bytes=64)
+        nc.vector.memset(xs2[:], 0.0)
+
+        spread = bank(7, [P, BLK, P])
+        for j in range(BLK):
+            nc.tensor.transpose(spread[:, j, :], margin_cols[:, j : j + 1].to_broadcast([P, P]), ident[:])
+        margin_rows = sb.tile([P, I], F32, name="margin_rows")
+        nc.scalar.copy(
+            out=margin_rows[:].rearrange("q (p j) -> q p j", j=BLK), in_=spread[:].rearrange("q j p -> q p j")
+        )
+
+        a = scores(hid_codes, hid_scale, 0, "a")
+        dhid_codes, dhid_scale = quantise(dhid_raw, "dhid")
+
+        half = sb.tile([P, 1], F32, name="half")
+        peak = sb.tile([P, 1], F32, name="peak")
+        neg_peak = sb.tile([P, 1], F32, name="neg_peak")
+        nc.scalar.activation(half[:], steep_col[:], ACT.Copy, scale=0.5)
+        nc.scalar.activation(peak[:], half[:], ACT.Square)
+        nc.scalar.activation(neg_peak[:], peak[:], ACT.Copy, scale=-1.0)
+
+        ta = scores(dhid_codes, dhid_scale, 4, "ta")
+
+        lower = sb.tile([P, I], F32, name="lower")
+        gap = sb.tile([P, I], F32, name="gap")
+        nc.vector.tensor_tensor(lower[:], a[:].indirect(first[:]), margin_rows[:], ALU.subtract)
+        nc.vector.tensor_tensor(gap[:], a[:].indirect(second[:]), lower[:], ALU.subtract)
+        th = sb.tile([P, I], F32, name="th")
+        th2 = sb.tile([P, I], F32, name="th2")
+        curv = sb.tile([P, I], F32, name="curv")
+        neg_curv = sb.tile([P, I], F32, name="neg_curv")
+        nc.scalar.activation(th[:], gap[:], ACT.Tanh, scale=half[:])
+        nc.scalar.activation(th2[:], th[:], ACT.Square)
+        nc.scalar.activation(curv[:], th2[:], ACT.Identity, scale=neg_peak[:], bias=peak[:])
+        nc.scalar.activation(neg_curv[:], th2[:], ACT.Identity, scale=peak[:], bias=neg_peak[:])
+
+        ta_first = sb.tile([P, I], F32, name="ta_first")
+        xb = sb.tile([P, I], F32, name="xb")
+        nc.vector.tensor_copy(ta_first[:], ta[:].indirect(first[:]))
+        nc.vector.tensor_tensor(xb[:], ta[:].indirect(second[:]), ta_first[:], ALU.subtract)
+
+        turned = []
+        for c in range(NCH):
+            t = bank(4 + c, [P, BLK, P])
+            for j in range(BLK):
+                nc.tensor.matmul(
+                    t[:, j, :], base_sb[c][:, j * P : (j + 1) * P], ident[:],
+                    start=(j == 0), stop=False, is_transpose=True,
+                )
+            turned.append(t)
+
+        nc.vector.tensor_tensor(xs1[:].indirect(second[:]), xb[:], curv[:], ALU.mult)
+        nc.vector.tensor_tensor(xs2[:].indirect(first[:]), xb[:], neg_curv[:], ALU.mult)
+
+        for c in range(NCH):
+            for j in range(BLK):
+                col = c * CH + j * P
+                nc.tensor.matmul(
+                    turned[c][:, j, :], xs1[:, col : col + P], ident[:],
+                    start=False, stop=(j == BLK - 1), is_transpose=True,
+                )
+            summed = sb.tile([P, BLK, P], F32, name="summed%d" % c)
+            nc.scalar.copy(out=summed[:], in_=turned[c][:])
+            back = bank(c, [P, CH])
+            for j in range(BLK):
+                nc.tensor.transpose(back[:, j * P : (j + 1) * P], summed[:, j, :], ident[:])
+            result = sb.tile([P, CH], F32, name="result%d" % c)
+            nc.vector.tensor_tensor(result[:], back[:], xs2[:, c * CH : (c + 1) * CH], ALU.add)
+            nc.sync.dma_start(out=out[:, c * CH : (c + 1) * CH], in_=result[:])

@@ -21,6 +21,7 @@ PACK = 4
 CH = 512
 NCH = V // CH
 BLK = CH // P
+NPE = NCH - 1
 
 
 def tile_attend_hvpairmargin_heads_kernel(tc, hid, voc_words, voc_scales, margin, steep, dhid, base, offs, offs2, out):
@@ -33,29 +34,33 @@ def tile_attend_hvpairmargin_heads_kernel(tc, hid, voc_words, voc_scales, margin
         def bank(b, shape):
             return ps.tile(shape, F32, name="bank%d" % b)
 
-        planes = sb.tile([P, CH], U8, name="planes", align_bytes=64)
-        nc.gpsimd.memset(planes[:].bitcast(I32), 0)
+        landed = sb.tile([P, CH // 4], I32, name="landed")
         scales_i32 = voc_scales[0].bitcast(I32)
         for quad in range(4):
             nc.scalar.dma_start(
-                out=planes[32 * quad : 32 * quad + 16, :].bitcast(I32),
+                out=landed[32 * quad : 32 * quad + 16, :],
                 in_=scales_i32[4 * quad : 4 * quad + 4, :].rearrange("r (c n) -> c r n", c=NCH),
             )
+        planes = sb.tile([P, CH], U8, name="planes", align_bytes=64)
+        nc.gpsimd.memset(planes[:].bitcast(I32), 0)
+        for quad in range(4):
+            rows = slice(32 * quad, 32 * quad + 16)
+            nc.vector.tensor_copy(planes[rows, :].bitcast(I32), landed[rows, :])
         warm = sb.tile([P, 1], F32, name="warm")
         warm_out = sb.tile([P, 1], F32, name="warm_out")
         nc.gpsimd.memset(warm[:], 0.0)
-        nc.scalar.activation(warm_out[:], warm[:], ACT.Tanh)
+        nc.scalar.activation(warm_out[:], warm[:], ACT.Sigmoid)
 
+        margin_cols = sb.tile([P, BLK], F32, name="margin_cols", tag="hid_scale", align_bytes=64)
+        nc.sync.dma_start(out=margin_cols[:], in_=margin[0].rearrange("(p j) -> p j", j=BLK))
         hid_raw = sb.tile([P, PACK, Q], F32, name="hid_raw")
         nc.sync.dma_start(out=hid_raw[:], in_=hid.rearrange("(p t) q -> p t q", t=PACK))
-        margin_cols = sb.tile([P, BLK], F32, name="margin_cols")
-        nc.sync.dma_start(out=margin_cols[:], in_=margin[0].rearrange("(p j) -> p j", j=BLK))
         words_i32 = voc_words[0].rearrange("p n t -> p (n t)").bitcast(I32)
         words = []
-        for c in range(NCH):
-            w = sb.tile([P, CH], U32, name="words%d" % c, align_bytes=64)
-            nc.sync.dma_start(out=w[:].bitcast(I32), in_=words_i32[:, c * CH : (c + 1) * CH])
-            words.append(w)
+        for h in range(2):
+            w = sb.tile([P, V // 2], U32, name="words%d" % h, align_bytes=64)
+            nc.sync.dma_start(out=w[:].bitcast(I32), in_=words_i32[:, h * (V // 2) : (h + 1) * (V // 2)])
+            words.extend([w[:, :CH], w[:, CH:]])
         dhid_raw = sb.tile([P, PACK, Q], F32, name="dhid_raw")
         nc.sync.dma_start(out=dhid_raw[:], in_=dhid.rearrange("(p t) q -> p t q", t=PACK))
         first = lists.tile([P, I // 16], U16, name="first")
@@ -76,10 +81,10 @@ def tile_attend_hvpairmargin_heads_kernel(tc, hid, voc_words, voc_scales, margin
         nc.vector.memset(xs1[:], 0.0)
 
         def quantise(raw, tag):
-            grouped = sb.tile([P, Q, PACK], BF16, name=tag + "_bf16", tag=tag + "_stage", align_bytes=64)
+            grouped = sb.tile([P, Q, PACK], BF16, name=tag + "_bf16", tag="stage", align_bytes=64)
             nc.vector.tensor_copy(out=grouped[:], in_=raw[:].rearrange("p t q -> p q t"))
-            codes = sb.tile([P, Q], U32, name=tag + "_codes", align_bytes=64)
-            scale = sb.tile([P, Q], U8, name=tag + "_scale", align_bytes=64)
+            codes = sb.tile([P, Q], U32, name=tag + "_codes", tag=tag + "_codes", align_bytes=64)
+            scale = sb.tile([P, Q], U8, name=tag + "_scale", tag=tag + "_scale", align_bytes=64)
             nc.vector.quantize_mx(
                 out=codes[:].bitcast(FP8X4), scales=scale[:], in_=grouped[:].rearrange("p q t -> p (q t)")
             )
@@ -93,7 +98,7 @@ def tile_attend_hvpairmargin_heads_kernel(tc, hid, voc_words, voc_scales, margin
                     out=acc[:],
                     lhsT=codes[:].bitcast(FP8X4),
                     lhsT_scale=scale[:],
-                    rhs=words[c][:].bitcast(FP8X4),
+                    rhs=words[c].bitcast(FP8X4),
                     rhs_scale=planes[4 * c : P, :],
                     start=True,
                     stop=True,
@@ -101,9 +106,6 @@ def tile_attend_hvpairmargin_heads_kernel(tc, hid, voc_words, voc_scales, margin
                 nc.scalar.copy(out=table[:, c * CH : (c + 1) * CH], in_=acc[:])
             return table
 
-        hid_codes, hid_scale = quantise(hid_raw, "hid")
-        xs2 = sb.tile([P, V], F32, name="xs2", tag="hid_stage", align_bytes=64)
-        nc.vector.memset(xs2[:], 0.0)
 
         spread = bank(7, [P, BLK, P])
         for j in range(BLK):
@@ -113,15 +115,21 @@ def tile_attend_hvpairmargin_heads_kernel(tc, hid, voc_words, voc_scales, margin
             out=margin_rows[:].rearrange("q (p j) -> q p j", j=BLK), in_=spread[:].rearrange("q j p -> q p j")
         )
 
+        hid_codes, hid_scale = quantise(hid_raw, "hid")
         a = scores(hid_codes, hid_scale, 0, "a")
         dhid_codes, dhid_scale = quantise(dhid_raw, "dhid")
+        xs2 = sb.tile([P, V], F32, name="xs2", tag="stage", align_bytes=64)
+        nc.gpsimd.memset(xs2[:], 0.0)
 
-        half = sb.tile([P, 1], F32, name="half")
-        peak = sb.tile([P, 1], F32, name="peak")
-        neg_peak = sb.tile([P, 1], F32, name="neg_peak")
-        nc.scalar.activation(half[:], steep_col[:], ACT.Copy, scale=0.5)
-        nc.scalar.activation(peak[:], half[:], ACT.Square)
-        nc.scalar.activation(neg_peak[:], peak[:], ACT.Copy, scale=-1.0)
+        def steep_squared(factor, name):
+            col = sb.tile([P, 1], F32, name=name)
+            nc.gpsimd.tensor_scalar(col[:], steep_col[:], steep_col[:], factor, ALU.mult, ALU.mult)
+            return col
+
+        neg_sq = steep_squared(-1.0, "neg_sq")
+        peak = steep_squared(0.25, "peak")
+        sq = steep_squared(1.0, "sq")
+        neg_peak = steep_squared(-0.25, "neg_peak")
 
         ta = scores(dhid_codes, dhid_scale, 4, "ta")
 
@@ -129,14 +137,14 @@ def tile_attend_hvpairmargin_heads_kernel(tc, hid, voc_words, voc_scales, margin
         gap = sb.tile([P, I], F32, name="gap")
         nc.vector.tensor_tensor(lower[:], a[:].indirect(first[:]), margin_rows[:], ALU.subtract)
         nc.vector.tensor_tensor(gap[:], a[:].indirect(second[:]), lower[:], ALU.subtract)
-        th = sb.tile([P, I], F32, name="th")
+        th = sb.tile([P, I], F32, name="th", tag="dhid_codes", align_bytes=64)
         th2 = sb.tile([P, I], F32, name="th2")
         curv = sb.tile([P, I], F32, name="curv")
         neg_curv = sb.tile([P, I], F32, name="neg_curv")
-        nc.scalar.activation(th[:], gap[:], ACT.Tanh, scale=half[:])
-        nc.scalar.activation(th2[:], th[:], ACT.Square)
-        nc.scalar.activation(curv[:], th2[:], ACT.Identity, scale=neg_peak[:], bias=peak[:])
-        nc.scalar.activation(neg_curv[:], th2[:], ACT.Identity, scale=peak[:], bias=neg_peak[:])
+        nc.scalar.activation(th[:], gap[:], ACT.Sigmoid, scale=steep_col[:])
+        nc.scalar.activation(th2[:], th[:], ACT.Square, bias=-0.5)
+        nc.scalar.activation(curv[:], th2[:], ACT.Identity, scale=neg_sq[:], bias=peak[:])
+        nc.scalar.activation(neg_curv[:], th2[:], ACT.Identity, scale=sq[:], bias=neg_peak[:])
 
         ta_first = sb.tile([P, I], F32, name="ta_first")
         xb = sb.tile([P, I], F32, name="xb")
@@ -144,7 +152,7 @@ def tile_attend_hvpairmargin_heads_kernel(tc, hid, voc_words, voc_scales, margin
         nc.vector.tensor_tensor(xb[:], ta[:].indirect(second[:]), ta_first[:], ALU.subtract)
 
         turned = []
-        for c in range(NCH):
+        for c in range(NPE):
             t = bank(4 + c, [P, BLK, P])
             for j in range(BLK):
                 nc.tensor.matmul(
@@ -156,18 +164,32 @@ def tile_attend_hvpairmargin_heads_kernel(tc, hid, voc_words, voc_scales, margin
         nc.vector.tensor_tensor(xs1[:].indirect(second[:]), xb[:], curv[:], ALU.mult)
         nc.vector.tensor_tensor(xs2[:].indirect(first[:]), xb[:], neg_curv[:], ALU.mult)
 
-        for c in range(NCH):
+        backs = []
+        for c in range(NPE):
             for j in range(BLK):
                 col = c * CH + j * P
                 nc.tensor.matmul(
                     turned[c][:, j, :], xs1[:, col : col + P], ident[:],
                     start=False, stop=(j == BLK - 1), is_transpose=True,
                 )
-            summed = sb.tile([P, BLK, P], F32, name="summed%d" % c)
+            summed = sb.tile([P, BLK, P], F32, name="summed%d" % c, tag="summed%d" % c)
             nc.scalar.copy(out=summed[:], in_=turned[c][:])
             back = bank(c, [P, CH])
             for j in range(BLK):
                 nc.tensor.transpose(back[:, j * P : (j + 1) * P], summed[:, j, :], ident[:])
-            result = sb.tile([P, CH], F32, name="result%d" % c)
-            nc.vector.tensor_tensor(result[:], back[:], xs2[:, c * CH : (c + 1) * CH], ALU.add)
-            nc.sync.dma_start(out=out[:, c * CH : (c + 1) * CH], in_=result[:])
+            backs.append(back)
+
+        last = slice(NPE * CH, V)
+        partial = sb.tile([P, CH], F32, name="partial")
+        nc.gpsimd.tensor_tensor(partial[:], xs2[:, last], base_sb[NPE][:], ALU.add)
+
+        def finish(c, lhs, rhs, tag):
+            cols = slice(c * CH, (c + 1) * CH)
+            result = sb.tile([P, CH], F32, name="result%d" % c, tag=tag)
+            nc.vector.tensor_tensor(result[:], lhs[:], rhs[:, cols], ALU.add)
+            nc.sync.dma_start(out=out[:, cols], in_=result[:])
+
+        finish(0, backs[0], xs2, "result0")
+        finish(1, backs[1], xs2, "result1")
+        finish(NPE, partial, xs1, "summed1")
+        finish(2, backs[2], xs2, "result2")

@@ -34,10 +34,14 @@ def tile_attend_hvpairmargin_heads_kernel(tc, hid, voc_words, voc_scales, margin
         def bank(b, shape):
             return ps.tile(shape, F32, name="bank%d" % b)
 
+        hid_raw = sb.tile([P, PACK, Q], F32, name="hid_raw")
+        nc.scalar.dma_start(out=hid_raw[:], in_=hid.rearrange("(p t) q -> p t q", t=PACK))
+        margin_cols = sb.tile([P, BLK], F32, name="margin_cols", tag="hid_scale", align_bytes=64)
+        nc.sync.dma_start(out=margin_cols[:], in_=margin[0].rearrange("(p j) -> p j", j=BLK))
         landed = sb.tile([P, CH // 4], I32, name="landed")
         scales_i32 = voc_scales[0].bitcast(I32)
         for quad in range(4):
-            nc.scalar.dma_start(
+            nc.sync.dma_start(
                 out=landed[32 * quad : 32 * quad + 16, :],
                 in_=scales_i32[4 * quad : 4 * quad + 4, :].rearrange("r (c n) -> c r n", c=NCH),
             )
@@ -49,12 +53,8 @@ def tile_attend_hvpairmargin_heads_kernel(tc, hid, voc_words, voc_scales, margin
         warm = sb.tile([P, 1], F32, name="warm")
         warm_out = sb.tile([P, 1], F32, name="warm_out")
         nc.gpsimd.memset(warm[:], 0.0)
-        nc.scalar.activation(warm_out[:], warm[:], ACT.Sigmoid)
+        nc.scalar.activation(warm_out[:], warm[:], ACT.Tanh)
 
-        margin_cols = sb.tile([P, BLK], F32, name="margin_cols", tag="hid_scale", align_bytes=64)
-        nc.sync.dma_start(out=margin_cols[:], in_=margin[0].rearrange("(p j) -> p j", j=BLK))
-        hid_raw = sb.tile([P, PACK, Q], F32, name="hid_raw")
-        nc.sync.dma_start(out=hid_raw[:], in_=hid.rearrange("(p t) q -> p t q", t=PACK))
         words_i32 = voc_words[0].rearrange("p n t -> p (n t)").bitcast(I32)
         words = []
         for h in range(2):
@@ -121,15 +121,10 @@ def tile_attend_hvpairmargin_heads_kernel(tc, hid, voc_words, voc_scales, margin
         xs2 = sb.tile([P, V], F32, name="xs2", tag="stage", align_bytes=64)
         nc.gpsimd.memset(xs2[:], 0.0)
 
-        def steep_squared(factor, name):
-            col = sb.tile([P, 1], F32, name=name)
-            nc.gpsimd.tensor_scalar(col[:], steep_col[:], steep_col[:], factor, ALU.mult, ALU.mult)
-            return col
-
-        neg_sq = steep_squared(-1.0, "neg_sq")
-        peak = steep_squared(0.25, "peak")
-        sq = steep_squared(1.0, "sq")
-        neg_peak = steep_squared(-0.25, "neg_peak")
+        coef = sb.tile([P, 2], F32, name="coef", tag="hid_codes", align_bytes=64)
+        half, peak = coef[:, 0:1], coef[:, 1:2]
+        nc.scalar.activation(half, steep_col[:], ACT.Copy, scale=0.5)
+        nc.scalar.activation(peak, steep_col[:], ACT.Square, scale=0.5)
 
         ta = scores(dhid_codes, dhid_scale, 4, "ta")
 
@@ -141,10 +136,10 @@ def tile_attend_hvpairmargin_heads_kernel(tc, hid, voc_words, voc_scales, margin
         th2 = sb.tile([P, I], F32, name="th2")
         curv = sb.tile([P, I], F32, name="curv")
         neg_curv = sb.tile([P, I], F32, name="neg_curv")
-        nc.scalar.activation(th[:], gap[:], ACT.Sigmoid, scale=steep_col[:])
-        nc.scalar.activation(th2[:], th[:], ACT.Square, bias=-0.5)
-        nc.scalar.activation(curv[:], th2[:], ACT.Identity, scale=neg_sq[:], bias=peak[:])
-        nc.scalar.activation(neg_curv[:], th2[:], ACT.Identity, scale=sq[:], bias=neg_peak[:])
+        nc.scalar.activation(th[:], gap[:], ACT.Tanh, scale=half)
+        nc.scalar.activation(th2[:], th[:], ACT.Square, scale=half)
+        nc.scalar.activation(curv[:], th2[:], ACT.Identity, scale=-1.0, bias=peak)
+        nc.scalar.activation(neg_curv[:], curv[:], ACT.Copy, scale=-1.0)
 
         ta_first = sb.tile([P, I], F32, name="ta_first")
         xb = sb.tile([P, I], F32, name="xb")

@@ -80,9 +80,12 @@ def tile_attend_hvpairmargin_heads_kernel(tc, hid, voc_words, voc_scales, margin
         xs1 = sb.tile([P, V], F32, name="xs1")
         nc.vector.memset(xs1[:], 0.0)
 
-        def quantise(raw, tag):
+        def quantise(raw, tag, split):
             grouped = sb.tile([P, Q, PACK], BF16, name=tag + "_bf16", tag="stage", align_bytes=64)
-            nc.vector.tensor_copy(out=grouped[:], in_=raw[:].rearrange("p t q -> p q t"))
+            by_column = raw[:].rearrange("p t q -> p q t")
+            nc.vector.tensor_copy(out=grouped[:, :split, :], in_=by_column[:, :split, :])
+            if split < Q:
+                nc.scalar.copy(out=grouped[:, split:, :], in_=by_column[:, split:, :])
             codes = sb.tile([P, Q], U32, name=tag + "_codes", tag=tag + "_codes", align_bytes=64)
             scale = sb.tile([P, Q], U8, name=tag + "_scale", tag=tag + "_scale", align_bytes=64)
             nc.vector.quantize_mx(
@@ -90,22 +93,21 @@ def tile_attend_hvpairmargin_heads_kernel(tc, hid, voc_words, voc_scales, margin
             )
             return codes, scale
 
-        def scores(codes, scale, first_bank, name):
+        def scores(codes, scale, pieces, name):
             table = sb.tile([P, V], F32, name=name)
-            for c in range(NCH):
-                acc = bank(first_bank + c, [P, CH])
+            for b, c, lo, hi, copy in pieces:
+                acc = bank(b, [P, hi - lo])
                 nc.tensor.matmul_mx(
                     out=acc[:],
                     lhsT=codes[:].bitcast(FP8X4),
                     lhsT_scale=scale[:],
-                    rhs=words[c].bitcast(FP8X4),
-                    rhs_scale=planes[4 * c : P, :],
+                    rhs=words[c][:, lo:hi].bitcast(FP8X4),
+                    rhs_scale=planes[4 * c : P, lo:hi],
                     start=True,
                     stop=True,
                 )
-                nc.scalar.copy(out=table[:, c * CH : (c + 1) * CH], in_=acc[:])
+                copy(out=table[:, c * CH + lo : c * CH + hi], in_=acc[:])
             return table
-
 
         spread = bank(7, [P, BLK, P])
         for j in range(BLK):
@@ -115,9 +117,15 @@ def tile_attend_hvpairmargin_heads_kernel(tc, hid, voc_words, voc_scales, margin
             out=margin_rows[:].rearrange("q (p j) -> q p j", j=BLK), in_=spread[:].rearrange("q j p -> q p j")
         )
 
-        hid_codes, hid_scale = quantise(hid_raw, "hid")
-        a = scores(hid_codes, hid_scale, 0, "a")
-        dhid_codes, dhid_scale = quantise(dhid_raw, "dhid")
+        hid_codes, hid_scale = quantise(hid_raw, "hid", Q // 2)
+        a = scores(
+            hid_codes,
+            hid_scale,
+            [(c, c, 0, CH, nc.scalar.copy) for c in range(NCH - 1)]
+            + [(3, 3, 0, CH // 2, nc.scalar.copy), (7, 3, CH // 2, CH, nc.vector.tensor_copy)],
+            "a",
+        )
+        dhid_codes, dhid_scale = quantise(dhid_raw, "dhid", Q)
         xs2 = sb.tile([P, V], F32, name="xs2", tag="stage", align_bytes=64)
         nc.gpsimd.memset(xs2[:], 0.0)
 
@@ -126,7 +134,7 @@ def tile_attend_hvpairmargin_heads_kernel(tc, hid, voc_words, voc_scales, margin
         nc.scalar.activation(half, steep_col[:], ACT.Copy, scale=0.5)
         nc.scalar.activation(peak, steep_col[:], ACT.Square, scale=0.5)
 
-        ta = scores(dhid_codes, dhid_scale, 4, "ta")
+        ta = scores(dhid_codes, dhid_scale, [(4 + c, c, 0, CH, nc.scalar.copy) for c in range(NCH)], "ta")
 
         lower = sb.tile([P, I], F32, name="lower")
         gap = sb.tile([P, I], F32, name="gap")
@@ -174,17 +182,22 @@ def tile_attend_hvpairmargin_heads_kernel(tc, hid, voc_words, voc_scales, margin
                 nc.tensor.transpose(back[:, j * P : (j + 1) * P], summed[:, j, :], ident[:])
             backs.append(back)
 
-        last = slice(NPE * CH, V)
-        partial = sb.tile([P, CH], F32, name="partial")
-        nc.gpsimd.tensor_tensor(partial[:], xs2[:, last], base_sb[NPE][:], ALU.add)
+        last = NPE * CH
+        mid = CH // 2
+        partial = sb.tile([P, mid], F32, name="partial")
+        nc.gpsimd.tensor_tensor(partial[:], xs2[:, last : last + mid], base_sb[NPE][:, :mid], ALU.add)
 
-        def finish(c, lhs, rhs, tag):
+        def finish(c):
             cols = slice(c * CH, (c + 1) * CH)
-            result = sb.tile([P, CH], F32, name="result%d" % c, tag=tag)
-            nc.vector.tensor_tensor(result[:], lhs[:], rhs[:, cols], ALU.add)
+            result = sb.tile([P, CH], F32, name="result%d" % c)
+            nc.vector.tensor_tensor(result[:], backs[c][:], xs2[:, cols], ALU.add)
             nc.sync.dma_start(out=out[:, cols], in_=result[:])
 
-        finish(0, backs[0], xs2, "result0")
-        finish(1, backs[1], xs2, "result1")
-        finish(NPE, partial, xs1, "summed1")
-        finish(2, backs[2], xs2, "result2")
+        finish(0)
+        finish(1)
+        rest = sb.tile([P, CH], F32, name="rest", tag="summed1")
+        nc.vector.tensor_tensor(rest[:, mid:], xs2[:, last + mid :], base_sb[NPE][:, mid:], ALU.add)
+        nc.vector.tensor_tensor(rest[:, :mid], partial[:], xs1[:, last : last + mid], ALU.add)
+        nc.vector.tensor_tensor(rest[:, mid:], rest[:, mid:], xs1[:, last + mid :], ALU.add)
+        nc.sync.dma_start(out=out[:, last:], in_=rest[:])
+        finish(2)

from contextlib import ExitStack

import concourse.mybir as mybir
from concourse.masks import make_identity

D, V, Q, I = 512, 2048, 128, 512
FLOPS = 2 * 2 * D * Q * V

F32 = mybir.dt.float32
BF16 = mybir.dt.bfloat16
I32 = mybir.dt.int32
U32 = mybir.dt.uint32
U16 = mybir.dt.uint16
U8 = mybir.dt.uint8
FP8X4 = mybir.dt.float8_e4m3fn_x4
ACT = mybir.ActivationFunctionType
ALU = mybir.AluOpType

P = 128
PACK = 4
CH = 512
NCH = V // CH
BLK = CH // P
NPE = NCH - 1


def tile_attend_hvpairmargin_heads_kernel(tc, hid, voc_words, voc_scales, margin, steep, dhid, base, offs, offs2, out):
    nc = tc.nc
    with ExitStack() as ctx:
        lists = ctx.enter_context(tc.tile_pool(name="lists", bufs=1))
        sb = ctx.enter_context(tc.tile_pool(name="sb", bufs=1))
        ps = ctx.enter_context(tc.psum_pool(name="ps", bufs=1))

        def bank(b, shape):
            return ps.tile(shape, F32, name="bank%d" % b)

        hid_raw = sb.tile([P, PACK, Q], F32, name="hid_raw")
        nc.scalar.dma_start(out=hid_raw[:], in_=hid.rearrange("(p t) q -> p t q", t=PACK))
        margin_cols = sb.tile([P, BLK], F32, name="margin_cols", tag="hid_scale", align_bytes=64)
        nc.sync.dma_start(out=margin_cols[:], in_=margin[0].rearrange("(p j) -> p j", j=BLK))
        landed = sb.tile([P, CH // 4], I32, name="landed")
        scales_i32 = voc_scales[0].bitcast(I32)
        for quad in range(4):
            nc.sync.dma_start(
                out=landed[32 * quad : 32 * quad + 16, :],
                in_=scales_i32[4 * quad : 4 * quad + 4, :].rearrange("r (c n) -> c r n", c=NCH),
            )
        planes = sb.tile([P, CH], U8, name="planes", align_bytes=64)
        nc.gpsimd.memset(planes[:].bitcast(I32), 0)
        for quad in range(4):
            rows = slice(32 * quad, 32 * quad + 16)
            nc.vector.tensor_copy(planes[rows, :].bitcast(I32), landed[rows, :])
        warm = sb.tile([P, 1], F32, name="warm")
        warm_out = sb.tile([P, 1], F32, name="warm_out")
        nc.gpsimd.memset(warm[:], 0.0)
        nc.scalar.activation(warm_out[:], warm[:], ACT.Tanh)

        words_i32 = voc_words[0].rearrange("p n t -> p (n t)").bitcast(I32)
        words = []
        for h in range(2):
            w = sb.tile([P, V // 2], U32, name="words%d" % h, align_bytes=64)
            nc.sync.dma_start(out=w[:].bitcast(I32), in_=words_i32[:, h * (V // 2) : (h + 1) * (V // 2)])
            words.extend([w[:, :CH], w[:, CH:]])
        dhid_raw = sb.tile([P, PACK, Q], F32, name="dhid_raw")
        nc.sync.dma_start(out=dhid_raw[:], in_=dhid.rearrange("(p t) q -> p t q", t=PACK))
        first = lists.tile([P, I // 16], U16, name="first")
        nc.sync.dma_start(first[:], offs)
        second = lists.tile([P, I // 16], U16, name="second")
        nc.sync.dma_start(second[:], offs2)
        steep_col = sb.tile([P, 1], F32, name="steep_col")
        nc.sync.dma_start(out=steep_col[:], in_=steep)
        base_sb = []
        for c in range(NCH):
            t = sb.tile([P, CH], F32, name="base%d" % c)
            nc.sync.dma_start(out=t[:], in_=base[:, c * CH : (c + 1) * CH])
            base_sb.append(t)

        ident = sb.tile([P, P], F32, name="ident")
        make_identity(nc, ident[:])
        xs1 = sb.tile([P, V], F32, name="xs1")
        nc.vector.memset(xs1[:], 0.0)

        def quantise(raw, tag, split):
            grouped = sb.tile([P, Q, PACK], BF16, name=tag + "_bf16", tag="stage", align_bytes=64)
            by_column = raw[:].rearrange("p t q -> p q t")
            nc.vector.tensor_copy(out=grouped[:, :split, :], in_=by_column[:, :split, :])
            if split < Q:
                nc.scalar.copy(out=grouped[:, split:, :], in_=by_column[:, split:, :])
            codes = sb.tile([P, Q], U32, name=tag + "_codes", tag=tag + "_codes", align_bytes=64)
            scale = sb.tile([P, Q], U8, name=tag + "_scale", tag=tag + "_scale", align_bytes=64)
            nc.vector.quantize_mx(
                out=codes[:].bitcast(FP8X4), scales=scale[:], in_=grouped[:].rearrange("p q t -> p (q t)")
            )
            return codes, scale

        def scores(codes, scale, pieces, name):
            table = sb.tile([P, V], F32, name=name)
            for b, c, lo, hi, copy in pieces:
                acc = bank(b, [P, hi - lo])
                nc.tensor.matmul_mx(
                    out=acc[:],
                    lhsT=codes[:].bitcast(FP8X4),
                    lhsT_scale=scale[:],
                    rhs=words[c][:, lo:hi].bitcast(FP8X4),
                    rhs_scale=planes[4 * c : P, lo:hi],
                    start=True,
                    stop=True,
                )
                copy(out=table[:, c * CH + lo : c * CH + hi], in_=acc[:])
            return table

        spread = bank(7, [P, BLK, P])
        for j in range(BLK):
            nc.tensor.transpose(spread[:, j, :], margin_cols[:, j : j + 1].to_broadcast([P, P]), ident[:])
        margin_rows = sb.tile([P, I], F32, name="margin_rows")
        nc.scalar.copy(
            out=margin_rows[:].rearrange("q (p j) -> q p j", j=BLK), in_=spread[:].rearrange("q j p -> q p j")
        )

        hid_codes, hid_scale = quantise(hid_raw, "hid", Q // 2)
        a = scores(
            hid_codes,
            hid_scale,
            [(c, c, 0, CH, nc.scalar.copy) for c in range(NCH - 1)]
            + [(3, 3, 0, CH // 2, nc.scalar.copy), (7, 3, CH // 2, CH, nc.vector.tensor_copy)],
            "a",
        )
        dhid_codes, dhid_scale = quantise(dhid_raw, "dhid", Q)
        xs2 = sb.tile([P, V], F32, name="xs2", tag="stage", align_bytes=64)
        nc.gpsimd.memset(xs2[:], 0.0)

        coef = sb.tile([P, 2], F32, name="coef", tag="hid_codes", align_bytes=64)
        half, peak = coef[:, 0:1], coef[:, 1:2]
        nc.scalar.activation(half, steep_col[:], ACT.Copy, scale=0.5)
        nc.scalar.activation(peak, steep_col[:], ACT.Square, scale=0.5)

        ta = scores(dhid_codes, dhid_scale, [(4 + c, c, 0, CH, nc.scalar.copy) for c in range(NCH)], "ta")

        lower = sb.tile([P, I], F32, name="lower")
        gap = sb.tile([P, I], F32, name="gap")
        nc.vector.tensor_tensor(lower[:], a[:].indirect(first[:]), margin_rows[:], ALU.subtract)
        nc.vector.tensor_tensor(gap[:], a[:].indirect(second[:]), lower[:], ALU.subtract)
        th = sb.tile([P, I], F32, name="th", tag="dhid_codes", align_bytes=64)
        th2 = sb.tile([P, I], F32, name="th2")
        curv = sb.tile([P, I], F32, name="curv")
        neg_curv = sb.tile([P, I], F32, name="neg_curv")
        nc.scalar.activation(th[:], gap[:], ACT.Tanh, scale=half)
        nc.scalar.activation(th2[:], th[:], ACT.Square, scale=half)
        nc.scalar.activation(curv[:], th2[:], ACT.Identity, scale=-1.0, bias=peak)
        nc.scalar.activation(neg_curv[:], curv[:], ACT.Copy, scale=-1.0)

        ta_first = sb.tile([P, I], F32, name="ta_first")
        xb = sb.tile([P, I], F32, name="xb")
        nc.vector.tensor_copy(ta_first[:], ta[:].indirect(first[:]))
        nc.vector.tensor_tensor(xb[:], ta[:].indirect(second[:]), ta_first[:], ALU.subtract)

        turned = []
        for c in range(NPE):
            t = bank(4 + c, [P, BLK, P])
            for j in range(BLK):
                nc.tensor.matmul(
                    t[:, j, :], base_sb[c][:, j * P : (j + 1) * P], ident[:],
                    start=(j == 0), stop=False, is_transpose=True,
                )
            turned.append(t)

        nc.vector.tensor_tensor(xs1[:].indirect(second[:]), xb[:], curv[:], ALU.mult)
        nc.vector.tensor_tensor(xs2[:].indirect(first[:]), xb[:], neg_curv[:], ALU.mult)

        backs = []
        for c in range(NPE):
            for j in range(BLK):
                col = c * CH + j * P
                nc.tensor.matmul(
                    turned[c][:, j, :], xs1[:, col : col + P], ident[:],
                    start=False, stop=(j == BLK - 1), is_transpose=True,
                )
            summed = sb.tile([P, BLK, P], F32, name="summed%d" % c, tag="summed%d" % c)
            nc.scalar.copy(out=summed[:], in_=turned[c][:])
            back = bank(c, [P, CH])
            for j in range(BLK):
                nc.tensor.transpose(back[:, j * P : (j + 1) * P], summed[:, j, :], ident[:])
            backs.append(back)

        last = NPE * CH
        mid = CH // 2
        partial = sb.tile([P, mid], F32, name="partial")
        nc.gpsimd.tensor_tensor(partial[:], xs2[:, last : last + mid], base_sb[NPE][:, :mid], ALU.add)

        def finish(c):
            cols = slice(c * CH, (c + 1) * CH)
            result = sb.tile([P, CH], F32, name="result%d" % c)
            nc.vector.tensor_tensor(result[:], backs[c][:], xs2[:, cols], ALU.add)
            nc.sync.dma_start(out=out[:, cols], in_=result[:])

        finish(0)
        finish(1)
        rest = sb.tile([P, CH], F32, name="rest", tag="summed1")
        nc.vector.tensor_tensor(rest[:, mid:], xs2[:, last + mid :], base_sb[NPE][:, mid:], ALU.add)
        nc.vector.tensor_tensor(rest[:, :mid], partial[:], xs1[:, last : last + mid], ALU.add)
        nc.vector.tensor_tensor(rest[:, mid:], rest[:, mid:], xs1[:, last + mid :], ALU.add)
        nc.sync.dma_start(out=out[:, last:], in_=rest[:])
        finish(2)
